import numpy as np
import ml_dtypes


def mxq(x, axis, fmt="e4m3"):
    dtype, down = {"e4m3": (ml_dtypes.float8_e4m3fn, 7), "e5m2": (ml_dtypes.float8_e5m2, 14)}[fmt]
    v = np.moveaxis(np.asarray(x, np.float32).astype(ml_dtypes.bfloat16).astype(np.float64), axis, -1)
    blocks = v.reshape(v.shape[:-1] + (-1, 32))
    amax = np.abs(blocks).max(-1, keepdims=True)
    byte = np.maximum(np.where(amax > 0, np.frexp(amax)[1] - 1 + 127, 0) - down, 1)
    scale = np.exp2(byte - 127.0)
    codes = (blocks / scale).astype(np.float32).astype(dtype).astype(np.float64)
    return np.moveaxis((codes * scale).reshape(v.shape), -1, axis)


WIDE = False


def mx_kscale(k):
    if not WIDE:
        return np.ones(k)
    levels = np.array([30, -30])
    if k % 512:
        return np.exp2(np.random.permutation(np.resize(levels, k // 32))).repeat(32)
    a = np.empty((k // 512, 16))
    for p in range(k // 512):
        a[p, :8] = np.random.permutation(np.resize(levels, 8))
        for g in range(8):
            far = levels[np.abs(levels - a[p, g]) >= 10]
            a[p, g + 8] = far[np.random.randint(len(far))]
    return np.exp2(a.ravel()).repeat(32)


def f64(x):
    return np.asarray(x).astype(np.float64)


def striped(idx):
    return np.tile(np.asarray(idx).reshape(-1, 16).T, (8, 1)).astype(np.uint16)


def unstriped(offs):
    return offs[:16].T.reshape(-1).astype(np.int64)


E2M1 = np.array([0.0, 0.5, 1.0, 1.5, 2.0, 3.0, 4.0, 6.0, -0.0, -0.5, -1.0, -1.5, -2.0, -3.0, -4.0, -6.0])


def pack_weight(w, fmt):
    k, n = w.shape
    w = f64(np.asarray(w, np.float32).astype(ml_dtypes.bfloat16)).reshape(k // 32, 32, n)
    amax = np.abs(w).max(1)
    if fmt in ("e4m3", "e5m2"):
        byte = np.frexp(amax)[1] - 1 + 127 - (7 if fmt == "e4m3" else 14)
    else:
        mant, ex = np.frexp(amax / 6.0)
        byte = np.where(mant > 0.5, ex, ex - 1) + 127
    byte = np.clip(np.where(amax > 0, byte, 1), 1, 254)
    scaled = (w * np.exp2(127.0 - byte)[:, None, :]).reshape(k, n).astype(np.float32)
    by_word = np.ascontiguousarray(scaled.reshape(k // 512, 128, 4, n).transpose(0, 1, 3, 2))
    if fmt in ("e4m3", "e5m2"):
        words = by_word.astype(ml_dtypes.float8_e4m3fn if fmt == "e4m3" else ml_dtypes.float8_e5m2).view(np.uint8)
    else:
        c = by_word.astype(ml_dtypes.float4_e2m1fn).view(np.uint8) & 0xF
        words = (c[..., 0::2] | (c[..., 1::2] << 4)).reshape(k // 512, 128, 2 * n)
    return np.ascontiguousarray(words), np.ascontiguousarray(byte.astype(np.uint8).reshape(k // 512, 16, n))


def unpack_weight(words, scales, fmt):
    g, _, n = scales.shape
    words = np.ascontiguousarray(words).reshape(g, 128, n, -1)
    if fmt in ("e4m3", "e5m2"):
        vals = words.view(ml_dtypes.float8_e4m3fn if fmt == "e4m3" else ml_dtypes.float8_e5m2).astype(np.float64)
    else:
        nib = np.empty((g, 128, n, 4), np.uint8)
        nib[..., 0::2] = words & 0xF
        nib[..., 1::2] = words >> 4
        vals = E2M1[nib]
    vals = vals * np.repeat(np.exp2(scales.astype(np.float64) - 127.0), 8, axis=1)[..., None]
    return vals.transpose(0, 1, 3, 2).reshape(g * 512, n)


def e4m3fn_bytes(y):
    return np.clip(np.asarray(y, np.float64), -448.0, 448.0).astype(np.float32).astype(ml_dtypes.float8_e4m3fn).view(np.uint8)


def e4m3fn_values(b):
    return np.asarray(b, np.uint8).view(ml_dtypes.float8_e4m3fn).astype(np.float64)


K, T, J, R, D, U, O = 512, 1024, 256, 512, 2048, 512, 256


def setup_inputs():
    n = np.random.standard_normal
    idx = np.random.permutation(T)[:J]
    idx2 = np.random.permutation(D)[:U]
    idx3 = np.random.permutation(U)[:O]
    fk = mx_kscale(K)
    fr = mx_kscale(R)
    xtp = pack_weight(n((K, T)) / fk[:, None], "e2m1")
    wp = pack_weight(n((K, R)) * 1 / np.sqrt(K) * fk[:, None] * fr, "e5m2")
    return {
        "xt_words": xtp[0],
        "xt_scales": xtp[1],
        "w_words": wp[0],
        "w_scales": wp[1],
        "ca": e4m3fn_bytes(60.0 * n((R, D))),
        "st": (np.random.uniform(0.0002, 0.0006, (R, 1)) / fr[:, None]).astype(np.float32),
        "offs": striped(idx),
        "offs2": striped(idx2),
        "offs3": striped(idx3),
    }


def reference(xt_words, xt_scales, w_words, w_scales, ca, st, offs, offs2, offs3):
    idx = unstriped(offs)
    idx2 = unstriped(offs2)
    idx3 = unstriped(offs3)
    xtu = unpack_weight(xt_words, xt_scales, "e2m1")
    wu = unpack_weight(w_words, w_scales, "e5m2")
    xtidxg = xtu[:, idx]
    a = wu.T @ xtidxg
    k1 = e4m3fn_values(ca)[:, idx2] * f64(st)
    kp = k1[:, idx3]
    aq = mxq(a, 0, "e4m3")
    kpq = mxq(kp, 0, "e4m3")
    p = aq.T @ kpq
    return p

@@ -1,0 +1,156 @@
+from contextlib import ExitStack
+
+import concourse.mybir as mybir
+
+K, T, J, R, D, U, O = 512, 1024, 256, 512, 2048, 512, 256
+FLOPS = 2 * K * R * J + 2 * R * J * O
+
+F32 = mybir.dt.float32
+BF16 = mybir.dt.bfloat16
+I32 = mybir.dt.int32
+U32 = mybir.dt.uint32
+U16 = mybir.dt.uint16
+U8 = mybir.dt.uint8
+FP8 = mybir.dt.float8_e4m3fn
+E4M3X4 = mybir.dt.float8_e4m3fn_x4
+E5M2X4 = mybir.dt.float8_e5m2_x4
+E2M1X4 = mybir.dt.float4_e2m1fn_x4
+COPY = mybir.ActivationFunctionType.Copy
+MULT = mybir.AluOpType.mult
+
+P = 128
+PACK = 4
+HALF = 128
+STRIPE = 16
+
+
+def tile_list_twolevels_kernel(tc, xt_words, xt_scales, w_words, w_scales, ca, st, offs, offs2, offs3, out):
+    nc = tc.nc
+    with ExitStack() as ctx:
+        pool = ctx.enter_context(tc.tile_pool(name="held", bufs=1))
+        psum = ctx.enter_context(tc.psum_pool(name="psum", bufs=1))
+
+        def sb(name, shape, dtype):
+            return pool.tile(shape, dtype, name=name, align_bytes=64)
+
+        list_x = sb("list_x", [P, J // STRIPE], U16)
+        list_c = sb("list_c", [P, U // STRIPE], U16)
+        list_k = sb("list_k", [P, O // STRIPE], U16)
+        cache = [sb("cache%d" % t, [P, D], U8) for t in range(PACK)]
+        steps = sb("steps", [P, PACK], F32)
+        x_words = sb("x_words", [P, T], U16)
+        x_scales = sb("x_scales", [P, T], U8)
+        w_raw = sb("w_raw", [P, R], U32)
+        ws_raw = sb("ws_raw", [P, R], U8)
+
+        ca_rows = ca.rearrange("(p t) d -> t p d", t=PACK)
+
+        nc.vector.memset(ws_raw[:].bitcast(I32), 0)
+        nc.vector.memset(x_scales[:].bitcast(I32), 0)
+
+        nc.sync.dma_start(list_c[:], offs2)
+        nc.sync.dma_start(cache[0][:], ca_rows[0])
+        for q in range(4):
+            nc.scalar.dma_start(ws_raw[32 * q : 32 * q + 4, :].bitcast(I32), w_scales[0, 4 * q : 4 * q + 4, :].bitcast(I32))
+        nc.gpsimd.dma_start(steps[:], st.rearrange("(p t) one -> p (t one)", t=PACK))
+        nc.sync.dma_start(w_raw[:].bitcast(I32), w_words[0].rearrange("p c b -> p (c b)").bitcast(I32))
+        nc.sync.dma_start(cache[1][:], ca_rows[1])
+        nc.sync.dma_start(list_k[:], offs3)
+        nc.sync.dma_start(x_words[:].bitcast(I32), xt_words[0].bitcast(I32))
+        nc.sync.dma_start(list_x[:], offs)
+        for q in range(4):
+            nc.sync.dma_start(x_scales[32 * q : 32 * q + 4, :].bitcast(I32), xt_scales[0, 4 * q : 4 * q + 4, :].bitcast(I32))
+        nc.sync.dma_start(cache[2][:], ca_rows[2])
+        nc.sync.dma_start(cache[3][:], ca_rows[3])
+
+        w_dealt = sb("w_dealt", [P, R], U32)
+        ws_dealt = sb("ws_dealt", [P, R], U8)
+        nc.vector.tensor_copy(ws_dealt[:].rearrange("p (t m) -> p t m", t=PACK), ws_raw[:].rearrange("p (m t) -> p t m", t=PACK))
+        nc.scalar.copy(w_dealt[:].rearrange("p (t m) -> p m t", t=PACK), w_raw[:].rearrange("p (m t) -> p m t", t=PACK))
+
+        picked = [sb("picked%d" % t, [P, U], U8) for t in range(PACK)]
+        k1 = [sb("k1_%d" % t, [P, U], F32) for t in range(PACK)]
+        kp4 = sb("kp4", [P, PACK * O], BF16)
+
+        def pick(t, lo, hi):
+            nc.vector.tensor_copy(picked[t][:, lo:hi], cache[t][:].indirect(list_c[:, lo // STRIPE : hi // STRIPE]))
+
+        def widen_scalar(t, lo, hi):
+            nc.scalar.activation(k1[t][:, lo:hi], picked[t][:, lo:hi].bitcast(FP8), COPY, scale=steps[:, t : t + 1])
+
+        def widen_vector(t, lo, hi):
+            nc.vector.tensor_scalar(k1[t][:, lo:hi], picked[t][:, lo:hi].bitcast(FP8), steps[:, t : t + 1], None, MULT)
+
+        def read_scalar(t, lo, hi):
+            nc.scalar.activation(kp4[:, PACK * lo + t : PACK * hi : PACK], k1[t][:].indirect(list_k[:, lo // STRIPE : hi // STRIPE]), COPY)
+
+        def read_vector(t, lo, hi):
+            nc.vector.tensor_copy(kp4[:, PACK * lo + t : PACK * hi : PACK], k1[t][:].indirect(list_k[:, lo // STRIPE : hi // STRIPE]))
+
+        xg_words = sb("xg_words", [P, J], U16)
+        xg_scales = sb("xg_scales", [P, J], U8)
+        a4 = sb("a4", [P, J, PACK], BF16)
+        a_codes = sb("a_codes", [P, J], U32)
+        a_scales = sb("a_scales", [P, J], U8)
+
+        for t in (0, 1):
+            pick(t, 0, U)
+            widen_scalar(t, 0, U)
+            read_scalar(t, 0, O)
+
+        nc.vector.tensor_copy(xg_words[:], x_words[:].indirect(list_x[:]))
+        nc.vector.tensor_copy(xg_scales[:], x_scales[:].indirect(list_x[:]))
+        for h in range(J // HALF):
+            cols = slice(h * HALF, (h + 1) * HALF)
+            a_ps = psum.tile([P, PACK, HALF], F32, name="a_ps%d" % h)
+            for t in range(PACK):
+                rows = slice(t * P, (t + 1) * P)
+                nc.tensor.matmul_mx(
+                    a_ps[:, t, :],
+                    lhsT=w_dealt[:, rows].bitcast(E5M2X4),
+                    lhsT_scale=ws_dealt[:, rows],
+                    rhs=xg_words[:, cols].bitcast(E2M1X4),
+                    rhs_scale=xg_scales[:, cols],
+                    start=True,
+                    stop=True,
+                )
+            nc.scalar.copy(a4[:, cols, :], a_ps[:].rearrange("p t j -> p j t"))
+
+        pick(2, 0, U)
+        widen_scalar(2, 0, U)
+        read_scalar(2, 0, HALF)
+        pick(3, 0, U // 2)
+        widen_scalar(3, 0, U // 2)
+        nc.vector.quantize_mx(a_codes[:].bitcast(E4M3X4), a_scales[:], a4[:].rearrange("p j t -> p (j t)"))
+        pick(3, U // 2, U)
+        read_vector(2, HALF, O)
+        widen_scalar(3, U // 2, U)
+        read_scalar(3, 0, HALF)
+        read_vector(3, HALF, O)
+
+        k_codes = sb("k_codes", [P, O], U32)
+        k_scales = sb("k_scales", [P, O], U8)
+        res = [sb("res%d" % h, [P, O], F32) for h in range(J // HALF)]
+        for g in range(O // HALF):
+            reads = slice(g * HALF, (g + 1) * HALF)
+            nc.vector.quantize_mx(
+                k_codes[:, reads].bitcast(E4M3X4), k_scales[:, reads], kp4[:, PACK * g * HALF : PACK * (g + 1) * HALF]
+            )
+            for h in range(J // HALF):
+                cols = slice(h * HALF, (h + 1) * HALF)
+                o_ps = psum.tile([P, HALF], F32, name="o_ps%d%d" % (g, h))
+                nc.tensor.matmul_mx(
+                    o_ps[:],
+                    lhsT=a_codes[:, cols].bitcast(E4M3X4),
+                    lhsT_scale=a_scales[:, cols],
+                    rhs=k_codes[:, reads].bitcast(E4M3X4),
+                    rhs_scale=k_scales[:, reads],
+                    start=True,
+                    stop=True,
+                )
+                if h == 0:
+                    nc.scalar.copy(res[h][:, reads], o_ps[:])
+                else:
+                    nc.vector.tensor_copy(res[h][:, reads], o_ps[:])
+        nc.scalar.dma_start(out[0:HALF, :], res[0][:])
+        nc.sync.dma_start(out[HALF:J, :], res[1][:])

@@ -47,6 +47,10 @@ def tile_list_twolevels_kernel(tc, xt_words, xt_scales, w_words, w_scales, ca, s
 
         nc.vector.memset(ws_raw[:].bitcast(I32), 0)
         nc.vector.memset(x_scales[:].bitcast(I32), 0)
+        warm_in = sb("warm_in", [P, 1], F32)
+        warm_out = sb("warm_out", [P, 1], F32)
+        nc.vector.memset(warm_in[:], 0.0)
+        nc.scalar.activation(warm_out[:], warm_in[:], COPY)
 
         nc.sync.dma_start(list_c[:], offs2)
         nc.sync.dma_start(cache[0][:], ca_rows[0])

@@ -52,10 +52,10 @@ def tile_list_twolevels_kernel(tc, xt_words, xt_scales, w_words, w_scales, ca, s
         nc.vector.memset(warm_in[:], 0.0)
         nc.scalar.activation(warm_out[:], warm_in[:], COPY)
 
-        nc.sync.dma_start(list_c[:], offs2)
         nc.sync.dma_start(cache[0][:], ca_rows[0])
+        nc.sync.dma_start(list_c[:], offs2)
         for q in range(4):
-            nc.scalar.dma_start(ws_raw[32 * q : 32 * q + 4, :].bitcast(I32), w_scales[0, 4 * q : 4 * q + 4, :].bitcast(I32))
+            nc.sync.dma_start(ws_raw[32 * q : 32 * q + 4, :].bitcast(I32), w_scales[0, 4 * q : 4 * q + 4, :].bitcast(I32))
         nc.gpsimd.dma_start(steps[:], st.rearrange("(p t) one -> p (t one)", t=PACK))
         nc.sync.dma_start(w_raw[:].bitcast(I32), w_words[0].rearrange("p c b -> p (c b)").bitcast(I32))
         nc.sync.dma_start(cache[1][:], ca_rows[1])
@@ -69,7 +69,7 @@ def tile_list_twolevels_kernel(tc, xt_words, xt_scales, w_words, w_scales, ca, s
 
         w_dealt = sb("w_dealt", [P, R], U32)
         ws_dealt = sb("ws_dealt", [P, R], U8)
-        nc.vector.tensor_copy(ws_dealt[:].rearrange("p (t m) -> p t m", t=PACK), ws_raw[:].rearrange("p (m t) -> p t m", t=PACK))
+        nc.gpsimd.tensor_copy(ws_dealt[:].rearrange("p (t m) -> p t m", t=PACK), ws_raw[:].rearrange("p (m t) -> p t m", t=PACK))
         nc.scalar.copy(w_dealt[:].rearrange("p (t m) -> p m t", t=PACK), w_raw[:].rearrange("p (m t) -> p m t", t=PACK))
 
         picked = [sb("picked%d" % t, [P, U], U8) for t in range(PACK)]
@@ -103,9 +103,9 @@ def tile_list_twolevels_kernel(tc, xt_words, xt_scales, w_words, w_scales, ca, s
             read_scalar(t, 0, O)
 
         nc.vector.tensor_copy(xg_words[:], x_words[:].indirect(list_x[:]))
-        nc.vector.tensor_copy(xg_scales[:], x_scales[:].indirect(list_x[:]))
         for h in range(J // HALF):
             cols = slice(h * HALF, (h + 1) * HALF)
+            nc.vector.tensor_copy(xg_scales[:, cols], x_scales[:].indirect(list_x[:, h * HALF // STRIPE : (h + 1) * HALF // STRIPE]))
             a_ps = psum.tile([P, PACK, HALF], F32, name="a_ps%d" % h)
             for t in range(PACK):
                 rows = slice(t * P, (t + 1) * P)
@@ -125,10 +125,10 @@ def tile_list_twolevels_kernel(tc, xt_words, xt_scales, w_words, w_scales, ca, s
         read_scalar(2, 0, HALF)
         pick(3, 0, U // 2)
         widen_scalar(3, 0, U // 2)
-        nc.vector.quantize_mx(a_codes[:].bitcast(E4M3X4), a_scales[:], a4[:].rearrange("p j t -> p (j t)"))
         pick(3, U // 2, U)
+        widen_vector(3, U // 2, U)
+        nc.vector.quantize_mx(a_codes[:].bitcast(E4M3X4), a_scales[:], a4[:].rearrange("p j t -> p (j t)"))
         read_vector(2, HALF, O)
-        widen_scalar(3, U // 2, U)
         read_scalar(3, 0, HALF)
         read_vector(3, HALF, O)
 
@@ -154,7 +154,7 @@ def tile_list_twolevels_kernel(tc, xt_words, xt_scales, w_words, w_scales, ca, s
                 )
                 if h == 0:
                     nc.scalar.copy(res[h][:, reads], o_ps[:])
+                    nc.scalar.dma_start(out[cols, reads], res[h][:, reads])
                 else:
                     nc.vector.tensor_copy(res[h][:, reads], o_ps[:])
-        nc.scalar.dma_start(out[0:HALF, :], res[0][:])
-        nc.sync.dma_start(out[HALF:J, :], res[1][:])
+                    nc.sync.dma_start(out[cols, reads], res[h][:, reads])

@@ -22,6 +22,8 @@ P = 128
 PACK = 4
 HALF = 128
 STRIPE = 16
+QUADRANT = 32
+SCALE_ROWS = 4
 
 
 def tile_list_twolevels_kernel(tc, xt_words, xt_scales, w_words, w_scales, ca, st, offs, offs2, offs3, out):
@@ -33,6 +35,16 @@ def tile_list_twolevels_kernel(tc, xt_words, xt_scales, w_words, w_scales, ca, s
         def sb(name, shape, dtype):
             return pool.tile(shape, dtype, name=name, align_bytes=64)
 
+        def entries(list_tile, lo, hi):
+            return list_tile[:, lo // STRIPE : hi // STRIPE]
+
+        def load_scale_rows(tile, scales):
+            for q in range(P // QUADRANT):
+                nc.sync.dma_start(
+                    tile[QUADRANT * q : QUADRANT * q + SCALE_ROWS, :].bitcast(I32),
+                    scales[0, SCALE_ROWS * q : SCALE_ROWS * (q + 1), :].bitcast(I32),
+                )
+
         list_x = sb("list_x", [P, J // STRIPE], U16)
         list_c = sb("list_c", [P, U // STRIPE], U16)
         list_k = sb("list_k", [P, O // STRIPE], U16)
@@ -43,53 +55,54 @@ def tile_list_twolevels_kernel(tc, xt_words, xt_scales, w_words, w_scales, ca, s
         w_raw = sb("w_raw", [P, R], U32)
         ws_raw = sb("ws_raw", [P, R], U8)
 
-        ca_rows = ca.rearrange("(p t) d -> t p d", t=PACK)
+        ca_planes = ca.rearrange("(p t) d -> t p d", t=PACK)
 
         nc.vector.memset(ws_raw[:].bitcast(I32), 0)
         nc.vector.memset(x_scales[:].bitcast(I32), 0)
+
         warm_in = sb("warm_in", [P, 1], F32)
         warm_out = sb("warm_out", [P, 1], F32)
         nc.vector.memset(warm_in[:], 0.0)
         nc.scalar.activation(warm_out[:], warm_in[:], COPY)
 
-        nc.sync.dma_start(cache[0][:], ca_rows[0])
+        nc.sync.dma_start(cache[0][:], ca_planes[0])
         nc.sync.dma_start(list_c[:], offs2)
-        for q in range(4):
-            nc.sync.dma_start(ws_raw[32 * q : 32 * q + 4, :].bitcast(I32), w_scales[0, 4 * q : 4 * q + 4, :].bitcast(I32))
+        load_scale_rows(ws_raw, w_scales)
         nc.gpsimd.dma_start(steps[:], st.rearrange("(p t) one -> p (t one)", t=PACK))
         nc.sync.dma_start(w_raw[:].bitcast(I32), w_words[0].rearrange("p c b -> p (c b)").bitcast(I32))
-        nc.sync.dma_start(cache[1][:], ca_rows[1])
+        nc.sync.dma_start(cache[1][:], ca_planes[1])
         nc.sync.dma_start(list_k[:], offs3)
         nc.sync.dma_start(x_words[:].bitcast(I32), xt_words[0].bitcast(I32))
         nc.sync.dma_start(list_x[:], offs)
-        for q in range(4):
-            nc.sync.dma_start(x_scales[32 * q : 32 * q + 4, :].bitcast(I32), xt_scales[0, 4 * q : 4 * q + 4, :].bitcast(I32))
-        nc.sync.dma_start(cache[2][:], ca_rows[2])
-        nc.sync.dma_start(cache[3][:], ca_rows[3])
+        load_scale_rows(x_scales, xt_scales)
+        nc.sync.dma_start(cache[2][:], ca_planes[2])
+        nc.sync.dma_start(cache[3][:], ca_planes[3])
 
         w_dealt = sb("w_dealt", [P, R], U32)
         ws_dealt = sb("ws_dealt", [P, R], U8)
-        nc.gpsimd.tensor_copy(ws_dealt[:].rearrange("p (t m) -> p t m", t=PACK), ws_raw[:].rearrange("p (m t) -> p t m", t=PACK))
+        nc.vector.tensor_copy(
+            ws_dealt[:].rearrange("p (t m) -> p t m", t=PACK), ws_raw[:].rearrange("p (m t) -> p t m", t=PACK)
+        )
         nc.scalar.copy(w_dealt[:].rearrange("p (t m) -> p m t", t=PACK), w_raw[:].rearrange("p (m t) -> p m t", t=PACK))
 
         picked = [sb("picked%d" % t, [P, U], U8) for t in range(PACK)]
         k1 = [sb("k1_%d" % t, [P, U], F32) for t in range(PACK)]
         kp4 = sb("kp4", [P, PACK * O], BF16)
 
-        def pick(t, lo, hi):
-            nc.vector.tensor_copy(picked[t][:, lo:hi], cache[t][:].indirect(list_c[:, lo // STRIPE : hi // STRIPE]))
+        def pick(t):
+            nc.vector.tensor_copy(picked[t][:], cache[t][:].indirect(list_c[:]))
 
-        def widen_scalar(t, lo, hi):
-            nc.scalar.activation(k1[t][:, lo:hi], picked[t][:, lo:hi].bitcast(FP8), COPY, scale=steps[:, t : t + 1])
+        def widen_on_scalar(t):
+            nc.scalar.activation(k1[t][:], picked[t][:].bitcast(FP8), COPY, scale=steps[:, t : t + 1])
 
-        def widen_vector(t, lo, hi):
-            nc.vector.tensor_scalar(k1[t][:, lo:hi], picked[t][:, lo:hi].bitcast(FP8), steps[:, t : t + 1], None, MULT)
+        def widen_on_vector(t):
+            nc.vector.tensor_scalar(k1[t][:], picked[t][:].bitcast(FP8), steps[:, t : t + 1], None, MULT)
 
-        def read_scalar(t, lo, hi):
-            nc.scalar.activation(kp4[:, PACK * lo + t : PACK * hi : PACK], k1[t][:].indirect(list_k[:, lo // STRIPE : hi // STRIPE]), COPY)
+        def read_on_scalar(t, lo, hi):
+            nc.scalar.activation(kp4[:, PACK * lo + t : PACK * hi : PACK], k1[t][:].indirect(entries(list_k, lo, hi)), COPY)
 
-        def read_vector(t, lo, hi):
-            nc.vector.tensor_copy(kp4[:, PACK * lo + t : PACK * hi : PACK], k1[t][:].indirect(list_k[:, lo // STRIPE : hi // STRIPE]))
+        def read_on_vector(t, lo, hi):
+            nc.vector.tensor_copy(kp4[:, PACK * lo + t : PACK * hi : PACK], k1[t][:].indirect(entries(list_k, lo, hi)))
 
         xg_words = sb("xg_words", [P, J], U16)
         xg_scales = sb("xg_scales", [P, J], U8)
@@ -97,64 +110,61 @@ def tile_list_twolevels_kernel(tc, xt_words, xt_scales, w_words, w_scales, ca, s
         a_codes = sb("a_codes", [P, J], U32)
         a_scales = sb("a_scales", [P, J], U8)
 
-        for t in (0, 1):
-            pick(t, 0, U)
-            widen_scalar(t, 0, U)
-            read_scalar(t, 0, O)
+        for t in range(PACK // 2):
+            pick(t)
+            widen_on_scalar(t)
+            read_on_scalar(t, 0, O)
 
         nc.vector.tensor_copy(xg_words[:], x_words[:].indirect(list_x[:]))
         for h in range(J // HALF):
-            cols = slice(h * HALF, (h + 1) * HALF)
-            nc.vector.tensor_copy(xg_scales[:, cols], x_scales[:].indirect(list_x[:, h * HALF // STRIPE : (h + 1) * HALF // STRIPE]))
+            slots = slice(h * HALF, (h + 1) * HALF)
+            nc.vector.tensor_copy(xg_scales[:, slots], x_scales[:].indirect(entries(list_x, slots.start, slots.stop)))
             a_ps = psum.tile([P, PACK, HALF], F32, name="a_ps%d" % h)
             for t in range(PACK):
-                rows = slice(t * P, (t + 1) * P)
+                plane = slice(t * P, (t + 1) * P)
                 nc.tensor.matmul_mx(
                     a_ps[:, t, :],
-                    lhsT=w_dealt[:, rows].bitcast(E5M2X4),
-                    lhsT_scale=ws_dealt[:, rows],
-                    rhs=xg_words[:, cols].bitcast(E2M1X4),
-                    rhs_scale=xg_scales[:, cols],
+                    lhsT=w_dealt[:, plane].bitcast(E5M2X4),
+                    lhsT_scale=ws_dealt[:, plane],
+                    rhs=xg_words[:, slots].bitcast(E2M1X4),
+                    rhs_scale=xg_scales[:, slots],
                     start=True,
                     stop=True,
                 )
-            nc.scalar.copy(a4[:, cols, :], a_ps[:].rearrange("p t j -> p j t"))
+            nc.scalar.copy(a4[:, slots, :], a_ps[:].rearrange("p t j -> p j t"))
 
-        pick(2, 0, U)
-        widen_scalar(2, 0, U)
-        read_scalar(2, 0, HALF)
-        pick(3, 0, U // 2)
-        widen_scalar(3, 0, U // 2)
-        pick(3, U // 2, U)
-        widen_vector(3, U // 2, U)
+        second_last, last = PACK - 2, PACK - 1
+        pick(second_last)
+        widen_on_scalar(second_last)
+        read_on_scalar(second_last, 0, HALF)
+        pick(last)
+        widen_on_vector(last)
         nc.vector.quantize_mx(a_codes[:].bitcast(E4M3X4), a_scales[:], a4[:].rearrange("p j t -> p (j t)"))
-        read_vector(2, HALF, O)
-        read_scalar(3, 0, HALF)
-        read_vector(3, HALF, O)
+        read_on_vector(second_last, HALF, O)
+        read_on_scalar(last, 0, HALF)
+        read_on_vector(last, HALF, O)
 
         k_codes = sb("k_codes", [P, O], U32)
         k_scales = sb("k_scales", [P, O], U8)
         res = [sb("res%d" % h, [P, O], F32) for h in range(J // HALF)]
+        empty_bank = (nc.scalar.copy, nc.vector.tensor_copy)
+        store = (nc.scalar.dma_start, nc.sync.dma_start)
         for g in range(O // HALF):
             reads = slice(g * HALF, (g + 1) * HALF)
             nc.vector.quantize_mx(
-                k_codes[:, reads].bitcast(E4M3X4), k_scales[:, reads], kp4[:, PACK * g * HALF : PACK * (g + 1) * HALF]
+                k_codes[:, reads].bitcast(E4M3X4), k_scales[:, reads], kp4[:, PACK * reads.start : PACK * reads.stop]
             )
             for h in range(J // HALF):
-                cols = slice(h * HALF, (h + 1) * HALF)
+                slots = slice(h * HALF, (h + 1) * HALF)
                 o_ps = psum.tile([P, HALF], F32, name="o_ps%d%d" % (g, h))
                 nc.tensor.matmul_mx(
                     o_ps[:],
-                    lhsT=a_codes[:, cols].bitcast(E4M3X4),
-                    lhsT_scale=a_scales[:, cols],
+                    lhsT=a_codes[:, slots].bitcast(E4M3X4),
+                    lhsT_scale=a_scales[:, slots],
                     rhs=k_codes[:, reads].bitcast(E4M3X4),
                     rhs_scale=k_scales[:, reads],
                     start=True,
                     stop=True,
                 )
-                if h == 0:
-                    nc.scalar.copy(res[h][:, reads], o_ps[:])
-                    nc.scalar.dma_start(out[cols, reads], res[h][:, reads])
-                else:
-                    nc.vector.tensor_copy(res[h][:, reads], o_ps[:])
-                    nc.sync.dma_start(out[cols, reads], res[h][:, reads])
+                empty_bank[h](res[h][:, reads], o_ps[:])
+                store[h](out[slots, reads], res[h][:, reads])

from contextlib import ExitStack

import concourse.mybir as mybir

K, T, J, R, D, U, O = 512, 1024, 256, 512, 2048, 512, 256
FLOPS = 2 * K * R * J + 2 * R * J * O

F32 = mybir.dt.float32
BF16 = mybir.dt.bfloat16
I32 = mybir.dt.int32
U32 = mybir.dt.uint32
U16 = mybir.dt.uint16
U8 = mybir.dt.uint8
FP8 = mybir.dt.float8_e4m3fn
E4M3X4 = mybir.dt.float8_e4m3fn_x4
E5M2X4 = mybir.dt.float8_e5m2_x4
E2M1X4 = mybir.dt.float4_e2m1fn_x4
COPY = mybir.ActivationFunctionType.Copy
MULT = mybir.AluOpType.mult

P = 128
PACK = 4
HALF = 128
STRIPE = 16
QUADRANT = 32
SCALE_ROWS = 4


def tile_list_twolevels_kernel(tc, xt_words, xt_scales, w_words, w_scales, ca, st, offs, offs2, offs3, out):
    nc = tc.nc
    with ExitStack() as ctx:
        pool = ctx.enter_context(tc.tile_pool(name="held", bufs=1))
        psum = ctx.enter_context(tc.psum_pool(name="psum", bufs=1))

        def sb(name, shape, dtype):
            return pool.tile(shape, dtype, name=name, align_bytes=64)

        def entries(list_tile, lo, hi):
            return list_tile[:, lo // STRIPE : hi // STRIPE]

        def load_scale_rows(tile, scales):
            for q in range(P // QUADRANT):
                nc.sync.dma_start(
                    tile[QUADRANT * q : QUADRANT * q + SCALE_ROWS, :].bitcast(I32),
                    scales[0, SCALE_ROWS * q : SCALE_ROWS * (q + 1), :].bitcast(I32),
                )

        list_x = sb("list_x", [P, J // STRIPE], U16)
        list_c = sb("list_c", [P, U // STRIPE], U16)
        list_k = sb("list_k", [P, O // STRIPE], U16)
        cache = [sb("cache%d" % t, [P, D], U8) for t in range(PACK)]
        steps = sb("steps", [P, PACK], F32)
        x_words = sb("x_words", [P, T], U16)
        x_scales = sb("x_scales", [P, T], U8)
        w_raw = sb("w_raw", [P, R], U32)
        ws_raw = sb("ws_raw", [P, R], U8)

        ca_planes = ca.rearrange("(p t) d -> t p d", t=PACK)

        nc.vector.memset(ws_raw[:].bitcast(I32), 0)
        nc.vector.memset(x_scales[:].bitcast(I32), 0)

        warm_in = sb("warm_in", [P, 1], F32)
        warm_out = sb("warm_out", [P, 1], F32)
        nc.vector.memset(warm_in[:], 0.0)
        nc.scalar.activation(warm_out[:], warm_in[:], COPY)

        nc.sync.dma_start(cache[0][:], ca_planes[0])
        nc.sync.dma_start(list_c[:], offs2)
        load_scale_rows(ws_raw, w_scales)
        nc.gpsimd.dma_start(steps[:], st.rearrange("(p t) one -> p (t one)", t=PACK))
        nc.sync.dma_start(w_raw[:].bitcast(I32), w_words[0].rearrange("p c b -> p (c b)").bitcast(I32))
        nc.sync.dma_start(cache[1][:], ca_planes[1])
        nc.sync.dma_start(list_k[:], offs3)
        nc.sync.dma_start(x_words[:].bitcast(I32), xt_words[0].bitcast(I32))
        nc.sync.dma_start(list_x[:], offs)
        load_scale_rows(x_scales, xt_scales)
        nc.sync.dma_start(cache[2][:], ca_planes[2])
        nc.sync.dma_start(cache[3][:], ca_planes[3])

        w_dealt = sb("w_dealt", [P, R], U32)
        ws_dealt = sb("ws_dealt", [P, R], U8)
        nc.vector.tensor_copy(
            ws_dealt[:].rearrange("p (t m) -> p t m", t=PACK), ws_raw[:].rearrange("p (m t) -> p t m", t=PACK)
        )
        nc.scalar.copy(w_dealt[:].rearrange("p (t m) -> p m t", t=PACK), w_raw[:].rearrange("p (m t) -> p m t", t=PACK))

        picked = [sb("picked%d" % t, [P, U], U8) for t in range(PACK)]
        k1 = [sb("k1_%d" % t, [P, U], F32) for t in range(PACK)]
        kp4 = sb("kp4", [P, PACK * O], BF16)

        def pick(t):
            nc.vector.tensor_copy(picked[t][:], cache[t][:].indirect(list_c[:]))

        def widen_on_scalar(t):
            nc.scalar.activation(k1[t][:], picked[t][:].bitcast(FP8), COPY, scale=steps[:, t : t + 1])

        def widen_on_vector(t):
            nc.vector.tensor_scalar(k1[t][:], picked[t][:].bitcast(FP8), steps[:, t : t + 1], None, MULT)

        def read_on_scalar(t, lo, hi):
            nc.scalar.activation(kp4[:, PACK * lo + t : PACK * hi : PACK], k1[t][:].indirect(entries(list_k, lo, hi)), COPY)

        def read_on_vector(t, lo, hi):
            nc.vector.tensor_copy(kp4[:, PACK * lo + t : PACK * hi : PACK], k1[t][:].indirect(entries(list_k, lo, hi)))

        xg_words = sb("xg_words", [P, J], U16)
        xg_scales = sb("xg_scales", [P, J], U8)
        a4 = sb("a4", [P, J, PACK], BF16)
        a_codes = sb("a_codes", [P, J], U32)
        a_scales = sb("a_scales", [P, J], U8)

        for t in range(PACK // 2):
            pick(t)
            widen_on_scalar(t)
            read_on_scalar(t, 0, O)

        nc.vector.tensor_copy(xg_words[:], x_words[:].indirect(list_x[:]))
        for h in range(J // HALF):
            slots = slice(h * HALF, (h + 1) * HALF)
            nc.vector.tensor_copy(xg_scales[:, slots], x_scales[:].indirect(entries(list_x, slots.start, slots.stop)))
            a_ps = psum.tile([P, PACK, HALF], F32, name="a_ps%d" % h)
            for t in range(PACK):
                plane = slice(t * P, (t + 1) * P)
                nc.tensor.matmul_mx(
                    a_ps[:, t, :],
                    lhsT=w_dealt[:, plane].bitcast(E5M2X4),
                    lhsT_scale=ws_dealt[:, plane],
                    rhs=xg_words[:, slots].bitcast(E2M1X4),
                    rhs_scale=xg_scales[:, slots],
                    start=True,
                    stop=True,
                )
            nc.scalar.copy(a4[:, slots, :], a_ps[:].rearrange("p t j -> p j t"))

        second_last, last = PACK - 2, PACK - 1
        pick(second_last)
        widen_on_scalar(second_last)
        read_on_scalar(second_last, 0, HALF)
        pick(last)
        widen_on_vector(last)
        nc.vector.quantize_mx(a_codes[:].bitcast(E4M3X4), a_scales[:], a4[:].rearrange("p j t -> p (j t)"))
        read_on_vector(second_last, HALF, O)
        read_on_scalar(last, 0, HALF)
        read_on_vector(last, HALF, O)

        k_codes = sb("k_codes", [P, O], U32)
        k_scales = sb("k_scales", [P, O], U8)
        res = [sb("res%d" % h, [P, O], F32) for h in range(J // HALF)]
        empty_bank = (nc.scalar.copy, nc.vector.tensor_copy)
        store = (nc.scalar.dma_start, nc.sync.dma_start)
        for g in range(O // HALF):
            reads = slice(g * HALF, (g + 1) * HALF)
            nc.vector.quantize_mx(
                k_codes[:, reads].bitcast(E4M3X4), k_scales[:, reads], kp4[:, PACK * reads.start : PACK * reads.stop]
            )
            for h in range(J // HALF):
                slots = slice(h * HALF, (h + 1) * HALF)
                o_ps = psum.tile([P, HALF], F32, name="o_ps%d%d" % (g, h))
                nc.tensor.matmul_mx(
                    o_ps[:],
                    lhsT=a_codes[:, slots].bitcast(E4M3X4),
                    lhsT_scale=a_scales[:, slots],
                    rhs=k_codes[:, reads].bitcast(E4M3X4),
                    rhs_scale=k_scales[:, reads],
                    start=True,
                    stop=True,
                )
                empty_bank[h](res[h][:, reads], o_ps[:])
                store[h](out[slots, reads], res[h][:, reads])
